import numpy as np
import ml_dtypes


def mxq(x, axis, fmt="e4m3"):
    dtype, down = {"e4m3": (ml_dtypes.float8_e4m3fn, 7), "e5m2": (ml_dtypes.float8_e5m2, 14)}[fmt]
    v = np.moveaxis(np.asarray(x, np.float32).astype(ml_dtypes.bfloat16).astype(np.float64), axis, -1)
    blocks = v.reshape(v.shape[:-1] + (-1, 32))
    amax = np.abs(blocks).max(-1, keepdims=True)
    byte = np.maximum(np.where(amax > 0, np.frexp(amax)[1] - 1 + 127, 0) - down, 1)
    scale = np.exp2(byte - 127.0)
    codes = (blocks / scale).astype(np.float32).astype(dtype).astype(np.float64)
    return np.moveaxis((codes * scale).reshape(v.shape), -1, axis)


WIDE = False


def mx_kscale(k, group=512):
    if not WIDE:
        return np.ones(k)
    levels = np.array([18, -18])
    if group != 512:
        return np.exp2(np.random.permutation(np.resize(levels, k // group))).repeat(group)
    if k % 512:
        return np.exp2(np.random.permutation(np.resize(levels, k // 32))).repeat(32)
    a = np.empty((k // 512, 16))
    for p in range(k // 512):
        a[p, :8] = np.random.permutation(np.resize(levels, 8))
        for g in range(8):
            far = levels[np.abs(levels - a[p, g]) >= 10]
            a[p, g + 8] = far[np.random.randint(len(far))]
    return np.exp2(a.ravel()).repeat(32)


def f64(x):
    return np.asarray(x).astype(np.float64)


def sigmoid(v):
    return 1.0 / (1.0 + np.exp(-v))


G, D, M, N = 4, 128, 128, 512


def setup_inputs():
    n = np.random.standard_normal
    s_d = mx_kscale(D, 0)
    return {
        "x": (n((G, D, N)) * s_d[:, None]).astype(np.float32),
        "w1": (n((G, D, M)) / np.sqrt(D) / s_d[:, None]).astype(np.float32),
        "w2": (n((G, D, M)) / np.sqrt(D) / s_d[:, None]).astype(np.float32),
        "tp": (np.random.uniform(0.5, 1.2, (G, M, 1))).astype(np.float32),
        "dx": (n((G, D, N)) * s_d[:, None]).astype(np.float32),
        "og": (np.random.uniform(0.5, 2.0, (G, M, 1))).astype(np.float32),
        "base": (0.3 * n((G, M, N))).astype(np.float32),
    }


def reference(x, w1, w2, tp, dx, og, base):
    w1q = mxq(f64(w1), 1, "e4m3")
    xq = mxq(f64(x), 1, "e4m3")
    z1 = w1q.transpose(0, 2, 1) @ xq
    dxq = mxq(f64(dx), 1, "e4m3")
    tz1 = w1q.transpose(0, 2, 1) @ dxq
    w2q = mxq(f64(w2), 1, "e4m3")
    z2 = w2q.transpose(0, 2, 1) @ xq
    tz2 = w2q.transpose(0, 2, 1) @ dxq
    s1 = z1 * f64(tp)
    ls = np.log(np.sum(np.exp(s1), axis=-1, keepdims=True))
    xs1 = tz1 * f64(tp)
    xls = np.sum(xs1 * np.exp(s1), axis=-1, keepdims=True) / np.sum(np.exp(s1), axis=-1, keepdims=True)
    xh = (xs1 - xls) * sigmoid(z2) + tz2 * sigmoid(z2) * (1.0 - sigmoid(z2)) * (s1 - ls + 6.0)
    y = xh * f64(og) + f64(base)
    return y

@@ -1,0 +1,196 @@
+import math
+from contextlib import ExitStack
+
+import concourse.mybir as mybir
+
+G, D, M, N = 4, 128, 128, 512
+FLOPS = 4 * 2 * G * D * M * N
+
+F32 = mybir.dt.float32
+BF16 = mybir.dt.bfloat16
+U32 = mybir.dt.uint32
+U8 = mybir.dt.uint8
+FP8X4 = mybir.dt.float8_e4m3fn_x4
+ALU = mybir.AluOpType
+ACT = mybir.ActivationFunctionType
+
+P = 128
+PACK = 4
+ROWS = D // PACK
+HALF = N // 2
+SCALAR_COLS = 128
+
+
+def tile_rows_tnrowlog_kernel(tc, x, w1, w2, tp, dx, og, base, out):
+    nc = tc.nc
+    groups = range(G)
+
+    with ExitStack() as ctx:
+        sb = ctx.enter_context(tc.tile_pool(name="sb", bufs=1))
+        ps = ctx.enter_context(tc.psum_pool(name="ps", bufs=1))
+        ctx.enter_context(tc.manual_schedule())
+
+        def operand(name, width):
+            raw = sb.tile([P, PACK, width], F32, name=name + "_raw", align_bytes=64)
+            packed = sb.tile([P, width, PACK], BF16, name=name + "_packed", align_bytes=64)
+            codes = sb.tile([P, width], U32, name=name + "_codes", align_bytes=64)
+            scales = sb.tile([P, width], U8, name=name + "_scales", align_bytes=64)
+            return raw, packed, codes, scales
+
+        def load(op, src):
+            nc.sync.dma_start(out=op[0][:], in_=src.rearrange("g (p j) n -> (g p) j n", j=PACK))
+
+        def interleave(copy, op, lo, hi):
+            raw, packed = op[0], op[1]
+            copy(
+                out=packed[:, lo:hi, :].rearrange("p (c i) j -> p c j i", i=4),
+                in_=raw[:, :, lo:hi].rearrange("p j (c i) -> p c j i", i=4),
+            )
+
+        def quantize(op, lo, hi):
+            packed, codes, scales = op[1], op[2], op[3]
+            nc.vector.quantize_mx(
+                out=codes[:, lo:hi].bitcast(FP8X4),
+                scales=scales[:, lo:hi],
+                in_=packed[:, lo:hi, :].rearrange("p c j -> p (c j)"),
+            )
+
+        def product(bank, w, a, g, passes=1):
+            rows = slice(ROWS * g, ROWS * (g + 1))
+            for i in range(passes):
+                nc.tensor.matmul_mx(
+                    out=bank[:],
+                    lhsT=w[2][rows, :].bitcast(FP8X4),
+                    lhsT_scale=w[3][rows, :],
+                    rhs=a[2][rows, :].bitcast(FP8X4),
+                    rhs_scale=a[3][rows, :],
+                    start=(i == 0),
+                    stop=(i == passes - 1),
+                )
+
+        def rows_of(name):
+            return [sb.tile([M, N], F32, name="%s%d" % (name, g)) for g in groups]
+
+        def stat(name):
+            return sb.tile([M, G], F32, name=name)
+
+        w1q, w2q = operand("w1", M), operand("w2", M)
+        xq, dxq = operand("x", N), operand("dx", N)
+        bank_a = [ps.tile([M, N], F32, name="bank_a%d" % g) for g in groups]
+        bank_b = [ps.tile([M, N], F32, name="bank_b%d" % g) for g in groups]
+        base_sb = sb.tile([M, G, N], F32)
+        e, t, h, sq, lg = rows_of("e"), rows_of("t"), rows_of("h"), rows_of("sq"), rows_of("lg")
+        lin, curv = rows_of("lin"), rows_of("curv")
+        gains_rows = sb.tile([P, 2 * M], F32, align_bytes=64)
+        gains = sb.tile([P, 2 * M], F32, align_bytes=64)
+        half_gain, og_m4, sum_e, sum_et, inv_e, mean, log_inv = (
+            stat(s) for s in ("half_gain", "og_m4", "sum_e", "sum_et", "inv_e", "mean", "log_inv")
+        )
+
+        nc.vector.memset(gains_rows[:], 0.0)
+        load(w1q, w1)
+        load(xq, x)
+        for i, vec in enumerate((tp, og)):
+            nc.sync.dma_start(
+                out=gains_rows[0:P:32, i * M : (i + 1) * M].rearrange("b (g r) -> b g r", g=G),
+                in_=vec.rearrange("g (b r) o -> b g (r o)", r=32),
+            )
+        load(dxq, dx)
+        load(w2q, w2)
+        nc.sync.dma_start(out=base_sb[:], in_=base.rearrange("g m n -> m g n"))
+
+        interleave(nc.scalar.copy, w1q, 0, M)
+        quantize(w1q, 0, M)
+
+        split = N - SCALAR_COLS
+        interleave(nc.vector.tensor_copy, xq, 0, HALF)
+        interleave(nc.vector.tensor_copy, xq, HALF, split)
+        interleave(nc.scalar.copy, xq, split, N)
+        quantize(xq, 0, HALF)
+        quantize(xq, HALF, N)
+        nc.vector.transpose(out=gains[:], in_=gains_rows[:])
+        tp_all, og_all = gains[:, 0:M:32], gains[:, M : 2 * M : 32]
+        tp_col = [gains[:, 32 * g : 32 * g + 1] for g in groups]
+        for g in groups:
+            product(bank_a[g], w1q, xq, g)
+            nc.scalar.activation(
+                out=e[g][:], in_=bank_a[g][:], func=ACT.Exp, scale=tp_col[g], accum_out=sum_e[:, g : g + 1]
+            )
+
+        interleave(nc.vector.tensor_copy, dxq, 0, HALF)
+        interleave(nc.vector.tensor_copy, dxq, HALF, N)
+        quantize(dxq, 0, HALF)
+        quantize(dxq, HALF, N)
+        for g in groups:
+            product(bank_b[g], w1q, dxq, g)
+        interleave(nc.vector.tensor_copy, w2q, 0, M)
+        nc.vector.scalar_tensor_tensor(
+            out=half_gain[:], in0=tp_all, scalar=0.5, in1=og_all, op0=ALU.mult, op1=ALU.mult
+        )
+        nc.vector.tensor_scalar(out=og_m4[:], in0=og_all, scalar1=-0.25, scalar2=None, op0=ALU.mult)
+        quantize(w2q, 0, M)
+        for g in groups:
+            product(bank_a[g], w2q, xq, g)
+
+        for g in groups:
+            nc.vector.scalar_tensor_tensor(
+                out=e[g][:], in0=bank_b[g][:], scalar=1.0, in1=e[g][:], op0=ALU.mult, op1=ALU.mult,
+                accum_out=sum_et[:, g : g + 1],
+            )
+            if g == G - 3:
+                nc.vector.reciprocal(out=inv_e[:], in_=sum_e[:])
+            if g == G - 2:
+                nc.vector.tensor_tensor(out=mean[:, 0:2], in0=sum_et[:, 0:2], in1=inv_e[:, 0:2], op=ALU.mult)
+            nc.scalar.activation(out=t[g][:], in_=bank_a[g][:], func=ACT.Tanh, scale=0.5)
+            product(bank_a[g], w1q, xq, g)
+            nc.gpsimd.tensor_scalar(
+                out=h[g][:], in0=t[g][:], scalar1=half_gain[:, g : g + 1], scalar2=half_gain[:, g : g + 1],
+                op0=ALU.mult, op1=ALU.add,
+            )
+
+        for g in groups:
+            nc.scalar.activation(out=sq[g][:], in_=t[g][:], func=ACT.Square)
+        nc.scalar.activation(out=log_inv[:], in_=inv_e[:], func=ACT.Ln, scale=math.exp(6.0))
+        for g in groups:
+            nc.scalar.activation(
+                out=lg[g][:], in_=bank_a[g][:], func=ACT.Identity, scale=tp_col[g], bias=log_inv[:, g : g + 1]
+            )
+
+        def add_base(eng, g):
+            eng.tensor_tensor(out=lin[g][:], in0=lin[g][:], in1=base_sb[:, g, :], op=ALU.add)
+
+        for g in groups:
+            nc.vector.scalar_tensor_tensor(
+                out=lin[g][:], in0=bank_b[g][:], scalar=mean[:, g : g + 1], in1=h[g][:],
+                op0=ALU.subtract, op1=ALU.mult,
+            )
+            if g == 0:
+                nc.vector.tensor_tensor(out=mean[:, 2:4], in0=sum_et[:, 2:4], in1=inv_e[:, 2:4], op=ALU.mult)
+            product(bank_b[g], w2q, dxq, g)
+            if g < G - 1:
+                add_base(nc.gpsimd, g)
+
+        for g in groups:
+            nc.vector.scalar_tensor_tensor(
+                out=curv[g][:], in0=sq[g][:], scalar=1.0, in1=bank_b[g][:], op0=ALU.subtract, op1=ALU.mult
+            )
+
+        def curve(g):
+            nc.vector.scalar_tensor_tensor(
+                out=curv[g][:], in0=lg[g][:], scalar=og_m4[:, g : g + 1], in1=curv[g][:],
+                op0=ALU.mult, op1=ALU.mult,
+            )
+
+        def finish(g):
+            nc.vector.tensor_tensor(out=lin[g][:], in0=lin[g][:], in1=curv[g][:], op=ALU.add)
+            nc.sync.dma_start(out=out[g], in_=lin[g][:])
+
+        curve(0)
+        add_base(nc.vector, G - 1)
+        finish(0)
+        curve(1)
+        curve(2)
+        finish(1)
+        curve(3)
+        finish(2)
+        finish(3)

@@ -18,7 +18,7 @@ P = 128
 PACK = 4
 ROWS = D // PACK
 HALF = N // 2
-SCALAR_COLS = 128
+SCALAR_COLS = 192
 
 
 def tile_rows_tnrowlog_kernel(tc, x, w1, w2, tp, dx, og, base, out):
@@ -30,25 +30,26 @@ def tile_rows_tnrowlog_kernel(tc, x, w1, w2, tp, dx, og, base, out):
         ps = ctx.enter_context(tc.psum_pool(name="ps", bufs=1))
         ctx.enter_context(tc.manual_schedule())
 
+        def raw_tile(name, width):
+            return sb.tile([P, PACK, width], F32, name=name + "_raw", align_bytes=64)
+
         def operand(name, width):
-            raw = sb.tile([P, PACK, width], F32, name=name + "_raw", align_bytes=64)
             packed = sb.tile([P, width, PACK], BF16, name=name + "_packed", align_bytes=64)
             codes = sb.tile([P, width], U32, name=name + "_codes", align_bytes=64)
             scales = sb.tile([P, width], U8, name=name + "_scales", align_bytes=64)
-            return raw, packed, codes, scales
+            return packed, codes, scales
 
-        def load(op, src):
-            nc.sync.dma_start(out=op[0][:], in_=src.rearrange("g (p j) n -> (g p) j n", j=PACK))
+        def load(raw, src):
+            nc.sync.dma_start(out=raw[:], in_=src.rearrange("g (p j) n -> (g p) j n", j=PACK))
 
-        def interleave(copy, op, lo, hi):
-            raw, packed = op[0], op[1]
+        def interleave(copy, op, lo, hi, raw):
             copy(
-                out=packed[:, lo:hi, :].rearrange("p (c i) j -> p c j i", i=4),
-                in_=raw[:, :, lo:hi].rearrange("p j (c i) -> p c j i", i=4),
+                out=op[0][:, lo:hi, :].rearrange("p (c i) j -> p c j i", i=4),
+                in_=raw.rearrange("p j (c i) -> p c j i", i=4),
             )
 
         def quantize(op, lo, hi):
-            packed, codes, scales = op[1], op[2], op[3]
+            packed, codes, scales = op
             nc.vector.quantize_mx(
                 out=codes[:, lo:hi].bitcast(FP8X4),
                 scales=scales[:, lo:hi],
@@ -60,10 +61,10 @@ def tile_rows_tnrowlog_kernel(tc, x, w1, w2, tp, dx, og, base, out):
             for i in range(passes):
                 nc.tensor.matmul_mx(
                     out=bank[:],
-                    lhsT=w[2][rows, :].bitcast(FP8X4),
-                    lhsT_scale=w[3][rows, :],
-                    rhs=a[2][rows, :].bitcast(FP8X4),
-                    rhs_scale=a[3][rows, :],
+                    lhsT=w[1][rows, :].bitcast(FP8X4),
+                    lhsT_scale=w[2][rows, :],
+                    rhs=a[1][rows, :].bitcast(FP8X4),
+                    rhs_scale=a[2][rows, :],
                     start=(i == 0),
                     stop=(i == passes - 1),
                 )
@@ -79,118 +80,155 @@ def tile_rows_tnrowlog_kernel(tc, x, w1, w2, tp, dx, og, base, out):
         bank_a = [ps.tile([M, N], F32, name="bank_a%d" % g) for g in groups]
         bank_b = [ps.tile([M, N], F32, name="bank_b%d" % g) for g in groups]
         base_sb = sb.tile([M, G, N], F32)
+        w1_raw, w2_raw, x_raw = raw_tile("w1", M), raw_tile("w2", M), raw_tile("x", N)
+        dx_raw = [raw_tile("dx%d" % i, HALF) for i in range(2)]
         e, t, h, sq, lg = rows_of("e"), rows_of("t"), rows_of("h"), rows_of("sq"), rows_of("lg")
         lin, curv = rows_of("lin"), rows_of("curv")
-        gains_rows = sb.tile([P, 2 * M], F32, align_bytes=64)
-        gains = sb.tile([P, 2 * M], F32, align_bytes=64)
-        half_gain, og_m4, sum_e, sum_et, inv_e, mean, log_inv = (
-            stat(s) for s in ("half_gain", "og_m4", "sum_e", "sum_et", "inv_e", "mean", "log_inv")
+        gains_rows = sb.tile([P, M], F32, align_bytes=64)
+        gains = sb.tile([P, M], F32, align_bytes=64)
+        half_gain, og_m4, sum_e, inv_e, mean, log_inv = (
+            stat(s) for s in ("half_gain", "og_m4", "sum_e", "inv_e", "mean", "log_inv")
         )
 
         nc.vector.memset(gains_rows[:], 0.0)
-        load(w1q, w1)
-        load(xq, x)
+        load(w1_raw, w1)
+        load(x_raw, x)
         for i, vec in enumerate((tp, og)):
             nc.sync.dma_start(
-                out=gains_rows[0:P:32, i * M : (i + 1) * M].rearrange("b (g r) -> b g r", g=G),
+                out=gains_rows[i:P:32, :].rearrange("b (g r) -> b g r", g=G),
                 in_=vec.rearrange("g (b r) o -> b g (r o)", r=32),
             )
-        load(dxq, dx)
-        load(w2q, w2)
+        load(w2_raw, w2)
+        for i in range(2):
+            load(dx_raw[i], dx[:, :, i * HALF : (i + 1) * HALF])
         nc.sync.dma_start(out=base_sb[:], in_=base.rearrange("g m n -> m g n"))
 
-        interleave(nc.scalar.copy, w1q, 0, M)
+        interleave(nc.scalar.copy, w1q, 0, M, w1_raw[:])
         quantize(w1q, 0, M)
 
         split = N - SCALAR_COLS
-        interleave(nc.vector.tensor_copy, xq, 0, HALF)
-        interleave(nc.vector.tensor_copy, xq, HALF, split)
-        interleave(nc.scalar.copy, xq, split, N)
+        interleave(nc.vector.tensor_copy, xq, 0, HALF, x_raw[:, :, 0:HALF])
+        interleave(nc.vector.tensor_copy, xq, HALF, split, x_raw[:, :, HALF:split])
+        interleave(nc.scalar.copy, xq, split, N, x_raw[:, :, split:N])
+        interleave(nc.scalar.copy, w2q, 0, M, w2_raw[:])
         quantize(xq, 0, HALF)
         quantize(xq, HALF, N)
         nc.vector.transpose(out=gains[:], in_=gains_rows[:])
-        tp_all, og_all = gains[:, 0:M:32], gains[:, M : 2 * M : 32]
+        quantize(w2q, 0, M)
+        tp_all, og_all = gains[:, 0:M:32], gains[:, 1:M:32]
         tp_col = [gains[:, 32 * g : 32 * g + 1] for g in groups]
-        for g in groups:
+
+        def col(tile, g):
+            return tile[:, g : g + 1]
+
+        def exp_rows(g):
             product(bank_a[g], w1q, xq, g)
             nc.scalar.activation(
-                out=e[g][:], in_=bank_a[g][:], func=ACT.Exp, scale=tp_col[g], accum_out=sum_e[:, g : g + 1]
+                out=e[g][:], in_=bank_a[g][:], func=ACT.Exp, scale=tp_col[g], accum_out=col(sum_e, g)
             )
 
-        interleave(nc.vector.tensor_copy, dxq, 0, HALF)
-        interleave(nc.vector.tensor_copy, dxq, HALF, N)
-        quantize(dxq, 0, HALF)
-        quantize(dxq, HALF, N)
-        for g in groups:
-            product(bank_b[g], w1q, dxq, g)
-        interleave(nc.vector.tensor_copy, w2q, 0, M)
-        nc.vector.scalar_tensor_tensor(
-            out=half_gain[:], in0=tp_all, scalar=0.5, in1=og_all, op0=ALU.mult, op1=ALU.mult
-        )
-        nc.vector.tensor_scalar(out=og_m4[:], in0=og_all, scalar1=-0.25, scalar2=None, op0=ALU.mult)
-        quantize(w2q, 0, M)
-        for g in groups:
-            product(bank_a[g], w2q, xq, g)
+        def tanh_rows(g):
+            product(bank_b[g], w2q, xq, g)
+            nc.scalar.activation(out=t[g][:], in_=bank_b[g][:], func=ACT.Tanh, scale=0.5)
 
-        for g in groups:
-            nc.vector.scalar_tensor_tensor(
-                out=e[g][:], in0=bank_b[g][:], scalar=1.0, in1=e[g][:], op0=ALU.mult, op1=ALU.mult,
-                accum_out=sum_et[:, g : g + 1],
-            )
-            if g == G - 3:
-                nc.vector.reciprocal(out=inv_e[:], in_=sum_e[:])
-            if g == G - 2:
-                nc.vector.tensor_tensor(out=mean[:, 0:2], in0=sum_et[:, 0:2], in1=inv_e[:, 0:2], op=ALU.mult)
-            nc.scalar.activation(out=t[g][:], in_=bank_a[g][:], func=ACT.Tanh, scale=0.5)
-            product(bank_a[g], w1q, xq, g)
+        def square(g):
+            nc.scalar.activation(out=sq[g][:], in_=t[g][:], func=ACT.Square)
+
+        def invert(g):
+            nc.vector.reciprocal(out=col(inv_e, g), in_=col(sum_e, g))
+
+        def gate(g):
             nc.gpsimd.tensor_scalar(
-                out=h[g][:], in0=t[g][:], scalar1=half_gain[:, g : g + 1], scalar2=half_gain[:, g : g + 1],
+                out=h[g][:], in0=t[g][:], scalar1=col(half_gain, g), scalar2=col(half_gain, g),
                 op0=ALU.mult, op1=ALU.add,
             )
 
-        for g in groups:
-            nc.scalar.activation(out=sq[g][:], in_=t[g][:], func=ACT.Square)
-        nc.scalar.activation(out=log_inv[:], in_=inv_e[:], func=ACT.Ln, scale=math.exp(6.0))
-        for g in groups:
-            nc.scalar.activation(
-                out=lg[g][:], in_=bank_a[g][:], func=ACT.Identity, scale=tp_col[g], bias=log_inv[:, g : g + 1]
+        def weighted_mean(g):
+            nc.vector.scalar_tensor_tensor(
+                out=e[g][:], in0=bank_b[g][:], scalar=col(inv_e, g), in1=e[g][:], op0=ALU.mult, op1=ALU.mult,
+                accum_out=col(mean, g),
             )
 
-        def add_base(eng, g):
-            eng.tensor_tensor(out=lin[g][:], in0=lin[g][:], in1=base_sb[:, g, :], op=ALU.add)
-
-        for g in groups:
+        def linear(g):
             nc.vector.scalar_tensor_tensor(
-                out=lin[g][:], in0=bank_b[g][:], scalar=mean[:, g : g + 1], in1=h[g][:],
+                out=lin[g][:], in0=bank_b[g][:], scalar=col(mean, g), in1=h[g][:],
                 op0=ALU.subtract, op1=ALU.mult,
             )
-            if g == 0:
-                nc.vector.tensor_tensor(out=mean[:, 2:4], in0=sum_et[:, 2:4], in1=inv_e[:, 2:4], op=ALU.mult)
             product(bank_b[g], w2q, dxq, g)
-            if g < G - 1:
-                add_base(nc.gpsimd, g)
+            nc.gpsimd.tensor_tensor(out=lin[g][:], in0=lin[g][:], in1=base_sb[:, g, :], op=ALU.add)
 
-        for g in groups:
+        def slope(g):
             nc.vector.scalar_tensor_tensor(
                 out=curv[g][:], in0=sq[g][:], scalar=1.0, in1=bank_b[g][:], op0=ALU.subtract, op1=ALU.mult
             )
 
-        def curve(g):
+        def curve(g, cols):
             nc.vector.scalar_tensor_tensor(
-                out=curv[g][:], in0=lg[g][:], scalar=og_m4[:, g : g + 1], in1=curv[g][:],
+                out=curv[g][:, cols], in0=lg[g][:, cols], scalar=col(og_m4, g), in1=curv[g][:, cols],
                 op0=ALU.mult, op1=ALU.mult,
             )
 
-        def finish(g):
-            nc.vector.tensor_tensor(out=lin[g][:], in0=lin[g][:], in1=curv[g][:], op=ALU.add)
-            nc.sync.dma_start(out=out[g], in_=lin[g][:])
+        def finish(g, cols):
+            nc.vector.tensor_tensor(out=lin[g][:, cols], in0=lin[g][:, cols], in1=curv[g][:, cols], op=ALU.add)
+            nc.sync.dma_start(out=out[g, :, cols], in_=lin[g][:, cols])
 
-        curve(0)
-        add_base(nc.vector, G - 1)
-        finish(0)
-        curve(1)
-        curve(2)
-        finish(1)
-        curve(3)
-        finish(2)
-        finish(3)
+        exp_rows(0)
+        tanh_rows(0)
+        exp_rows(1)
+        tanh_rows(1)
+        tanh_rows(2)
+
+        interleave(nc.vector.tensor_copy, dxq, 0, HALF, dx_raw[0][:])
+        nc.vector.tensor_scalar(out=og_m4[:], in0=og_all, scalar1=-0.25, scalar2=None, op0=ALU.mult)
+        quantize(dxq, 0, HALF)
+        interleave(nc.vector.tensor_copy, dxq, HALF, N, dx_raw[1][:])
+        invert(0)
+        quantize(dxq, HALF, N)
+        nc.vector.scalar_tensor_tensor(
+            out=half_gain[:], in0=tp_all, scalar=0.5, in1=og_all, op0=ALU.mult, op1=ALU.mult
+        )
+        invert(1)
+
+        product(bank_b[0], w1q, dxq, 0)
+        tanh_rows(3)
+        product(bank_b[1], w1q, dxq, 1)
+        exp_rows(2)
+        exp_rows(3)
+        product(bank_b[2], w1q, dxq, 2)
+        product(bank_b[3], w1q, dxq, 3)
+        for g in groups:
+            gate(g)
+        for g in groups[:-1]:
+            square(g)
+
+        weighted_mean(0)
+        weighted_mean(1)
+        linear(0)
+        invert(2)
+        linear(1)
+        invert(3)
+        weighted_mean(2)
+        weighted_mean(3)
+        linear(2)
+        linear(3)
+        nc.scalar.activation(out=log_inv[:], in_=inv_e[:], func=ACT.Ln, scale=math.exp(6.0))
+        square(3)
+        for g in groups:
+            slope(g)
+
+        for g in groups:
+            nc.scalar.activation(
+                out=lg[g][:], in_=bank_a[g][:], func=ACT.Identity, scale=tp_col[g], bias=col(log_inv, g)
+            )
+
+        whole, halves = slice(0, N), (slice(0, HALF), slice(HALF, N))
+        curve(0, whole)
+        curve(1, whole)
+        finish(0, whole)
+        curve(2, whole)
+        finish(1, whole)
+        finish(2, whole)
+        for cols in halves:
+            curve(3, cols)
+        for cols in halves:
+            finish(3, cols)

@@ -18,7 +18,8 @@ P = 128
 PACK = 4
 ROWS = D // PACK
 HALF = N // 2
-SCALAR_COLS = 192
+SCALAR_COLS = 128
+TINY = 1e-18
 
 
 def tile_rows_tnrowlog_kernel(tc, x, w1, w2, tp, dx, og, base, out):
@@ -82,17 +83,18 @@ def tile_rows_tnrowlog_kernel(tc, x, w1, w2, tp, dx, og, base, out):
         base_sb = sb.tile([M, G, N], F32)
         w1_raw, w2_raw, x_raw = raw_tile("w1", M), raw_tile("w2", M), raw_tile("x", N)
         dx_raw = [raw_tile("dx%d" % i, HALF) for i in range(2)]
-        e, t, h, sq, lg = rows_of("e"), rows_of("t"), rows_of("h"), rows_of("sq"), rows_of("lg")
+        e, t, h, sq = rows_of("e"), rows_of("t"), rows_of("h"), rows_of("sq")
         lin, curv = rows_of("lin"), rows_of("curv")
         gains_rows = sb.tile([P, M], F32, align_bytes=64)
         gains = sb.tile([P, M], F32, align_bytes=64)
-        half_gain, og_m4, sum_e, inv_e, mean, log_inv = (
-            stat(s) for s in ("half_gain", "og_m4", "sum_e", "inv_e", "mean", "log_inv")
+        half_gain, gain_m4, nudge, tp_safe, tp_inv = (
+            stat(s) for s in ("half_gain", "gain_m4", "nudge", "tp_safe", "tp_inv")
         )
+        sum_e, inv_e, mean, log_inv, shift = (stat(s) for s in ("sum_e", "inv_e", "mean", "log_inv", "shift"))
 
         nc.vector.memset(gains_rows[:], 0.0)
-        load(w1_raw, w1)
         load(x_raw, x)
+        load(w1_raw, w1)
         for i, vec in enumerate((tp, og)):
             nc.sync.dma_start(
                 out=gains_rows[i:P:32, :].rearrange("b (g r) -> b g r", g=G),
@@ -103,16 +105,15 @@ def tile_rows_tnrowlog_kernel(tc, x, w1, w2, tp, dx, og, base, out):
             load(dx_raw[i], dx[:, :, i * HALF : (i + 1) * HALF])
         nc.sync.dma_start(out=base_sb[:], in_=base.rearrange("g m n -> m g n"))
 
-        interleave(nc.scalar.copy, w1q, 0, M, w1_raw[:])
-        quantize(w1q, 0, M)
-
         split = N - SCALAR_COLS
         interleave(nc.vector.tensor_copy, xq, 0, HALF, x_raw[:, :, 0:HALF])
         interleave(nc.vector.tensor_copy, xq, HALF, split, x_raw[:, :, HALF:split])
         interleave(nc.scalar.copy, xq, split, N, x_raw[:, :, split:N])
+        interleave(nc.scalar.copy, w1q, 0, M, w1_raw[:])
         interleave(nc.scalar.copy, w2q, 0, M, w2_raw[:])
         quantize(xq, 0, HALF)
         quantize(xq, HALF, N)
+        quantize(w1q, 0, M)
         nc.vector.transpose(out=gains[:], in_=gains_rows[:])
         quantize(w2q, 0, M)
         tp_all, og_all = gains[:, 0:M:32], gains[:, 1:M:32]
@@ -164,12 +165,15 @@ def tile_rows_tnrowlog_kernel(tc, x, w1, w2, tp, dx, og, base, out):
 
         def curve(g, cols):
             nc.vector.scalar_tensor_tensor(
-                out=curv[g][:, cols], in0=lg[g][:, cols], scalar=col(og_m4, g), in1=curv[g][:, cols],
-                op0=ALU.mult, op1=ALU.mult,
+                out=curv[g][:, cols], in0=bank_a[g][:, cols], scalar=col(shift, g), in1=curv[g][:, cols],
+                op0=ALU.add, op1=ALU.mult,
             )
 
         def finish(g, cols):
-            nc.vector.tensor_tensor(out=lin[g][:, cols], in0=lin[g][:, cols], in1=curv[g][:, cols], op=ALU.add)
+            nc.vector.scalar_tensor_tensor(
+                out=lin[g][:, cols], in0=curv[g][:, cols], scalar=col(gain_m4, g), in1=lin[g][:, cols],
+                op0=ALU.mult, op1=ALU.add,
+            )
             nc.sync.dma_start(out=out[g, :, cols], in_=lin[g][:, cols])
 
         exp_rows(0)
@@ -178,16 +182,25 @@ def tile_rows_tnrowlog_kernel(tc, x, w1, w2, tp, dx, og, base, out):
         tanh_rows(1)
         tanh_rows(2)
 
+        nc.vector.tensor_scalar(
+            out=nudge[:], in0=tp_all, scalar1=0.0, scalar2=2 * TINY, op0=ALU.is_ge, op1=ALU.mult
+        )
         interleave(nc.vector.tensor_copy, dxq, 0, HALF, dx_raw[0][:])
-        nc.vector.tensor_scalar(out=og_m4[:], in0=og_all, scalar1=-0.25, scalar2=None, op0=ALU.mult)
+        nc.vector.scalar_tensor_tensor(
+            out=tp_safe[:], in0=nudge[:], scalar=TINY, in1=tp_all, op0=ALU.subtract, op1=ALU.add
+        )
         quantize(dxq, 0, HALF)
+        nc.vector.scalar_tensor_tensor(
+            out=gain_m4[:], in0=tp_safe[:], scalar=-0.25, in1=og_all, op0=ALU.mult, op1=ALU.mult
+        )
         interleave(nc.vector.tensor_copy, dxq, HALF, N, dx_raw[1][:])
         invert(0)
         quantize(dxq, HALF, N)
+        invert(1)
+        nc.vector.reciprocal(out=tp_inv[:], in_=tp_safe[:])
         nc.vector.scalar_tensor_tensor(
             out=half_gain[:], in0=tp_all, scalar=0.5, in1=og_all, op0=ALU.mult, op1=ALU.mult
         )
-        invert(1)
 
         product(bank_b[0], w1q, dxq, 0)
         tanh_rows(3)
@@ -198,8 +211,8 @@ def tile_rows_tnrowlog_kernel(tc, x, w1, w2, tp, dx, og, base, out):
         product(bank_b[3], w1q, dxq, 3)
         for g in groups:
             gate(g)
-        for g in groups[:-1]:
-            square(g)
+        square(0)
+        square(1)
 
         weighted_mean(0)
         weighted_mean(1)
@@ -212,18 +225,18 @@ def tile_rows_tnrowlog_kernel(tc, x, w1, w2, tp, dx, og, base, out):
         linear(2)
         linear(3)
         nc.scalar.activation(out=log_inv[:], in_=inv_e[:], func=ACT.Ln, scale=math.exp(6.0))
+        for g in groups:
+            nc.scalar.activation(out=col(shift, g), in_=col(log_inv, g), func=ACT.Identity, scale=col(tp_inv, g))
+        square(2)
         square(3)
-        for g in groups:
-            slope(g)
-
-        for g in groups:
-            nc.scalar.activation(
-                out=lg[g][:], in_=bank_a[g][:], func=ACT.Identity, scale=tp_col[g], bias=col(log_inv, g)
-            )
 
         whole, halves = slice(0, N), (slice(0, HALF), slice(HALF, N))
+        slope(0)
+        slope(1)
         curve(0, whole)
         curve(1, whole)
+        slope(2)
+        slope(3)
         finish(0, whole)
         curve(2, whole)
         finish(1, whole)

import math
from contextlib import ExitStack

import concourse.mybir as mybir

G, D, M, N = 4, 128, 128, 512
FLOPS = 4 * 2 * G * D * M * N

F32 = mybir.dt.float32
BF16 = mybir.dt.bfloat16
U32 = mybir.dt.uint32
U8 = mybir.dt.uint8
FP8X4 = mybir.dt.float8_e4m3fn_x4
ALU = mybir.AluOpType
ACT = mybir.ActivationFunctionType

P = 128
PACK = 4
ROWS = D // PACK
HALF = N // 2
SCALAR_COLS = 128
TINY = 1e-18


def tile_rows_tnrowlog_kernel(tc, x, w1, w2, tp, dx, og, base, out):
    nc = tc.nc
    groups = range(G)

    with ExitStack() as ctx:
        sb = ctx.enter_context(tc.tile_pool(name="sb", bufs=1))
        ps = ctx.enter_context(tc.psum_pool(name="ps", bufs=1))
        ctx.enter_context(tc.manual_schedule())

        def raw_tile(name, width):
            return sb.tile([P, PACK, width], F32, name=name + "_raw", align_bytes=64)

        def operand(name, width):
            packed = sb.tile([P, width, PACK], BF16, name=name + "_packed", align_bytes=64)
            codes = sb.tile([P, width], U32, name=name + "_codes", align_bytes=64)
            scales = sb.tile([P, width], U8, name=name + "_scales", align_bytes=64)
            return packed, codes, scales

        def load(raw, src):
            nc.sync.dma_start(out=raw[:], in_=src.rearrange("g (p j) n -> (g p) j n", j=PACK))

        def interleave(copy, op, lo, hi, raw):
            copy(
                out=op[0][:, lo:hi, :].rearrange("p (c i) j -> p c j i", i=4),
                in_=raw.rearrange("p j (c i) -> p c j i", i=4),
            )

        def quantize(op, lo, hi):
            packed, codes, scales = op
            nc.vector.quantize_mx(
                out=codes[:, lo:hi].bitcast(FP8X4),
                scales=scales[:, lo:hi],
                in_=packed[:, lo:hi, :].rearrange("p c j -> p (c j)"),
            )

        def product(bank, w, a, g, passes=1):
            rows = slice(ROWS * g, ROWS * (g + 1))
            for i in range(passes):
                nc.tensor.matmul_mx(
                    out=bank[:],
                    lhsT=w[1][rows, :].bitcast(FP8X4),
                    lhsT_scale=w[2][rows, :],
                    rhs=a[1][rows, :].bitcast(FP8X4),
                    rhs_scale=a[2][rows, :],
                    start=(i == 0),
                    stop=(i == passes - 1),
                )

        def rows_of(name):
            return [sb.tile([M, N], F32, name="%s%d" % (name, g)) for g in groups]

        def stat(name):
            return sb.tile([M, G], F32, name=name)

        w1q, w2q = operand("w1", M), operand("w2", M)
        xq, dxq = operand("x", N), operand("dx", N)
        bank_a = [ps.tile([M, N], F32, name="bank_a%d" % g) for g in groups]
        bank_b = [ps.tile([M, N], F32, name="bank_b%d" % g) for g in groups]
        base_sb = sb.tile([M, G, N], F32)
        w1_raw, w2_raw, x_raw = raw_tile("w1", M), raw_tile("w2", M), raw_tile("x", N)
        dx_raw = [raw_tile("dx%d" % i, HALF) for i in range(2)]
        e, t, h, sq = rows_of("e"), rows_of("t"), rows_of("h"), rows_of("sq")
        lin, curv = rows_of("lin"), rows_of("curv")
        gains_rows = sb.tile([P, M], F32, align_bytes=64)
        gains = sb.tile([P, M], F32, align_bytes=64)
        half_gain, gain_m4, nudge, tp_safe, tp_inv = (
            stat(s) for s in ("half_gain", "gain_m4", "nudge", "tp_safe", "tp_inv")
        )
        sum_e, inv_e, mean, log_inv, shift = (stat(s) for s in ("sum_e", "inv_e", "mean", "log_inv", "shift"))

        nc.vector.memset(gains_rows[:], 0.0)
        load(x_raw, x)
        load(w1_raw, w1)
        for i, vec in enumerate((tp, og)):
            nc.sync.dma_start(
                out=gains_rows[i:P:32, :].rearrange("b (g r) -> b g r", g=G),
                in_=vec.rearrange("g (b r) o -> b g (r o)", r=32),
            )
        load(w2_raw, w2)
        for i in range(2):
            load(dx_raw[i], dx[:, :, i * HALF : (i + 1) * HALF])
        nc.sync.dma_start(out=base_sb[:], in_=base.rearrange("g m n -> m g n"))

        split = N - SCALAR_COLS
        interleave(nc.vector.tensor_copy, xq, 0, HALF, x_raw[:, :, 0:HALF])
        interleave(nc.vector.tensor_copy, xq, HALF, split, x_raw[:, :, HALF:split])
        interleave(nc.scalar.copy, xq, split, N, x_raw[:, :, split:N])
        interleave(nc.scalar.copy, w1q, 0, M, w1_raw[:])
        interleave(nc.scalar.copy, w2q, 0, M, w2_raw[:])
        quantize(xq, 0, HALF)
        quantize(xq, HALF, N)
        quantize(w1q, 0, M)
        nc.vector.transpose(out=gains[:], in_=gains_rows[:])
        quantize(w2q, 0, M)
        tp_all, og_all = gains[:, 0:M:32], gains[:, 1:M:32]
        tp_col = [gains[:, 32 * g : 32 * g + 1] for g in groups]

        def col(tile, g):
            return tile[:, g : g + 1]

        def exp_rows(g):
            product(bank_a[g], w1q, xq, g)
            nc.scalar.activation(
                out=e[g][:], in_=bank_a[g][:], func=ACT.Exp, scale=tp_col[g], accum_out=col(sum_e, g)
            )

        def tanh_rows(g):
            product(bank_b[g], w2q, xq, g)
            nc.scalar.activation(out=t[g][:], in_=bank_b[g][:], func=ACT.Tanh, scale=0.5)

        def square(g):
            nc.scalar.activation(out=sq[g][:], in_=t[g][:], func=ACT.Square)

        def invert(g):
            nc.vector.reciprocal(out=col(inv_e, g), in_=col(sum_e, g))

        def gate(g):
            nc.gpsimd.tensor_scalar(
                out=h[g][:], in0=t[g][:], scalar1=col(half_gain, g), scalar2=col(half_gain, g),
                op0=ALU.mult, op1=ALU.add,
            )

        def weighted_mean(g):
            nc.vector.scalar_tensor_tensor(
                out=e[g][:], in0=bank_b[g][:], scalar=col(inv_e, g), in1=e[g][:], op0=ALU.mult, op1=ALU.mult,
                accum_out=col(mean, g),
            )

        def linear(g):
            nc.vector.scalar_tensor_tensor(
                out=lin[g][:], in0=bank_b[g][:], scalar=col(mean, g), in1=h[g][:],
                op0=ALU.subtract, op1=ALU.mult,
            )
            product(bank_b[g], w2q, dxq, g)
            nc.gpsimd.tensor_tensor(out=lin[g][:], in0=lin[g][:], in1=base_sb[:, g, :], op=ALU.add)

        def slope(g):
            nc.vector.scalar_tensor_tensor(
                out=curv[g][:], in0=sq[g][:], scalar=1.0, in1=bank_b[g][:], op0=ALU.subtract, op1=ALU.mult
            )

        def curve(g, cols):
            nc.vector.scalar_tensor_tensor(
                out=curv[g][:, cols], in0=bank_a[g][:, cols], scalar=col(shift, g), in1=curv[g][:, cols],
                op0=ALU.add, op1=ALU.mult,
            )

        def finish(g, cols):
            nc.vector.scalar_tensor_tensor(
                out=lin[g][:, cols], in0=curv[g][:, cols], scalar=col(gain_m4, g), in1=lin[g][:, cols],
                op0=ALU.mult, op1=ALU.add,
            )
            nc.sync.dma_start(out=out[g, :, cols], in_=lin[g][:, cols])

        exp_rows(0)
        tanh_rows(0)
        exp_rows(1)
        tanh_rows(1)
        tanh_rows(2)

        nc.vector.tensor_scalar(
            out=nudge[:], in0=tp_all, scalar1=0.0, scalar2=2 * TINY, op0=ALU.is_ge, op1=ALU.mult
        )
        interleave(nc.vector.tensor_copy, dxq, 0, HALF, dx_raw[0][:])
        nc.vector.scalar_tensor_tensor(
            out=tp_safe[:], in0=nudge[:], scalar=TINY, in1=tp_all, op0=ALU.subtract, op1=ALU.add
        )
        quantize(dxq, 0, HALF)
        nc.vector.scalar_tensor_tensor(
            out=gain_m4[:], in0=tp_safe[:], scalar=-0.25, in1=og_all, op0=ALU.mult, op1=ALU.mult
        )
        interleave(nc.vector.tensor_copy, dxq, HALF, N, dx_raw[1][:])
        invert(0)
        quantize(dxq, HALF, N)
        invert(1)
        nc.vector.reciprocal(out=tp_inv[:], in_=tp_safe[:])
        nc.vector.scalar_tensor_tensor(
            out=half_gain[:], in0=tp_all, scalar=0.5, in1=og_all, op0=ALU.mult, op1=ALU.mult
        )

        product(bank_b[0], w1q, dxq, 0)
        tanh_rows(3)
        product(bank_b[1], w1q, dxq, 1)
        exp_rows(2)
        exp_rows(3)
        product(bank_b[2], w1q, dxq, 2)
        product(bank_b[3], w1q, dxq, 3)
        for g in groups:
            gate(g)
        square(0)
        square(1)

        weighted_mean(0)
        weighted_mean(1)
        linear(0)
        invert(2)
        linear(1)
        invert(3)
        weighted_mean(2)
        weighted_mean(3)
        linear(2)
        linear(3)
        nc.scalar.activation(out=log_inv[:], in_=inv_e[:], func=ACT.Ln, scale=math.exp(6.0))
        for g in groups:
            nc.scalar.activation(out=col(shift, g), in_=col(log_inv, g), func=ACT.Identity, scale=col(tp_inv, g))
        square(2)
        square(3)

        whole, halves = slice(0, N), (slice(0, HALF), slice(HALF, N))
        slope(0)
        slope(1)
        curve(0, whole)
        curve(1, whole)
        slope(2)
        slope(3)
        finish(0, whole)
        curve(2, whole)
        finish(1, whole)
        finish(2, whole)
        for cols in halves:
            curve(3, cols)
        for cols in halves:
            finish(3, cols)
